import numpy as np
import ml_dtypes


def mxq(x, axis, fmt="e4m3"):
    dtype, down = {"e4m3": (ml_dtypes.float8_e4m3fn, 7), "e5m2": (ml_dtypes.float8_e5m2, 14)}[fmt]
    v = np.moveaxis(np.asarray(x, np.float32).astype(ml_dtypes.bfloat16).astype(np.float64), axis, -1)
    blocks = v.reshape(v.shape[:-1] + (-1, 32))
    amax = np.abs(blocks).max(-1, keepdims=True)
    byte = np.maximum(np.where(amax > 0, np.frexp(amax)[1] - 1 + 127, 0) - down, 1)
    scale = np.exp2(byte - 127.0)
    codes = (blocks / scale).astype(np.float32).astype(dtype).astype(np.float64)
    return np.moveaxis((codes * scale).reshape(v.shape), -1, axis)


WIDE = False


def mx_kscale(k):
    if not WIDE:
        return np.ones(k)
    levels = np.array([10, -10, 5, -5, 0])
    if k % 512:
        return np.exp2(np.random.permutation(np.resize(levels, k // 32))).repeat(32)
    a = np.empty((k // 512, 16))
    for p in range(k // 512):
        a[p, :8] = np.random.permutation(np.resize(levels, 8))
        for g in range(8):
            far = levels[np.abs(levels - a[p, g]) >= 10]
            a[p, g + 8] = far[np.random.randint(len(far))]
    return np.exp2(a.ravel()).repeat(32)


def f64(x):
    return np.asarray(x).astype(np.float64)


def striped(idx):
    return np.tile(idx.reshape(-1, 16).T, (8, 1)).astype(np.uint16)


def unstriped(offs):
    return offs[:16].T.reshape(-1).astype(np.int64)


def relu(v):
    return np.maximum(v, 0.0)


K, T, D, S, V, N = 512, 1024, 4, 2048, 512, 256


def setup_inputs():
    n = np.random.standard_normal
    s = mx_kscale(K)[:, None]
    return {
        "xT": (n((K, T)) * s).astype(np.float32),
        "w": (n((K, N)) / np.sqrt(K) / s).astype(np.float32),
        "b": (0.3 * n((N, 1))).astype(np.float32),
        "offs": striped(np.concatenate([np.random.permutation(T)[:V] for _ in range(D)])),
    }


def reference(xT, w, b, offs):
    idx = unstriped(offs)
    x = np.empty((K, V))
    for l in range(D):
        r = l // 4 * (4 * K // D) + l % 4 + 4 * np.arange(K // D)
        x[r] = f64(xT)[r][:, idx[l * V:(l + 1) * V]]
    xq = mxq(x, 0, "e4m3")
    return relu((mxq(f64(w), 0, "e4m3").T @ xq) + f64(b))

@@ -1,0 +1,117 @@
+from contextlib import ExitStack
+
+import concourse.mybir as mybir
+
+K, T, LEVELS, V, N = 512, 1024, 4, 512, 256
+FLOPS = 2 * K * V * N
+
+F32 = mybir.dt.float32
+BF16 = mybir.dt.bfloat16
+U32 = mybir.dt.uint32
+I32 = mybir.dt.int32
+U16 = mybir.dt.uint16
+U8 = mybir.dt.uint8
+FP8X4 = mybir.dt.float8_e4m3fn_x4
+RELU = mybir.ActivationFunctionType.Relu
+COPY = mybir.ActivationFunctionType.Copy
+ADD, MAX = mybir.AluOpType.add, mybir.AluOpType.max
+
+P = 128
+PACK = 4
+M_TILE = 128
+GROUP = 16
+CHUNKS = [(0, 256), (256, 512)]
+
+
+def interleave_views(dst, src):
+    return (
+        dst.rearrange("p (c i) t -> p c t i", i=4),
+        src.rearrange("p t (c i) -> p c t i", i=4),
+    )
+
+
+def tile_picked_grid_lin_relu_sub_l_kernel(tc, xT, w, b, offs, out):
+    nc = tc.nc
+    with ExitStack() as ctx:
+        keep = ctx.enter_context(tc.tile_pool(name="keep", bufs=1))
+        psum = ctx.enter_context(tc.psum_pool(name="psum", bufs=1))
+
+        offsets = keep.tile([P, LEVELS * V // GROUP], U16, name="offsets")
+        nc.sync.dma_start(offsets[:], offs)
+
+        def level_offsets(level, v0, v1):
+            return offsets[:, (level * V + v0) // GROUP : (level * V + v1) // GROUP]
+
+        levels = xT.rearrange("(f l) t -> l f t", l=LEVELS)
+        tables = [keep.tile([P, T], F32, name=f"table{l}") for l in range(LEVELS)]
+        w_raw = keep.tile([P, PACK, N], F32, name="w_raw")
+        bias = keep.tile([P, N // M_TILE], F32, name="bias")
+        for l in range(LEVELS):
+            nc.sync.dma_start(tables[l][:], levels[l])
+        nc.sync.dma_start(w_raw[:], w.rearrange("(p j) n -> p j n", j=PACK))
+        with nc.allow_non_contiguous_dma(reason="one bias value a partition"):
+            nc.sync.dma_start(bias[:], b.rearrange("(c p) o -> p (c o)", p=P))
+
+        zero = keep.tile([P, 1], F32, name="zero")
+        warm = keep.tile([P, 1], F32, name="warm")
+        nc.vector.memset(zero[:], 0.0)
+        nc.scalar.activation(warm[:], zero[:], RELU)
+
+        pairs = keep.tile([P, 2, V, 2], BF16, name="pairs")
+        for l in range(2):
+            rounded = keep.tile([P, T], BF16, name=f"rounded{l}")
+            nc.vector.tensor_copy(rounded[:], tables[l][:])
+            nc.scalar.activation(pairs[:, 0, :, l], rounded[:].indirect(level_offsets(l, 0, V)), COPY)
+        nc.vector.tensor_copy(pairs[:, 1, :, 0], tables[2][:].indirect(level_offsets(2, 0, V)))
+        for v0, v1 in CHUNKS:
+            l = LEVELS - 1
+            nc.vector.tensor_copy(pairs[:, l // 2, v0:v1, l % 2], tables[l][:].indirect(level_offsets(l, v0, v1)))
+        pair_words = pairs[:].rearrange("p u v e -> p u (v e)").bitcast(I32)
+
+        grouped = []
+        for c, (v0, v1) in enumerate(CHUNKS):
+            g = keep.tile([P, (v1 - v0) * PACK], BF16, name=f"grouped{c}", align_bytes=64)
+            nc.vector.tensor_copy(
+                g[:].bitcast(I32).rearrange("p (c i u) -> p c u i", i=4, u=2),
+                pair_words[:, :, v0:v1].rearrange("p u (c i) -> p c u i", i=4),
+            )
+            grouped.append(g)
+
+        w_grouped = []
+        for m in range(N // M_TILE):
+            g = keep.tile([P, M_TILE, PACK], BF16, name=f"w_grouped{m}", align_bytes=64)
+            nc.scalar.copy(*interleave_views(g[:], w_raw[:, :, m * M_TILE : (m + 1) * M_TILE]))
+            w_grouped.append(g)
+
+        def quantize(name, values):
+            n = values.shape[1] // PACK
+            codes = keep.tile([P, n], U32, name=f"{name}_codes", align_bytes=64)
+            scales = keep.tile([P, n], U8, name=f"{name}_scales", align_bytes=64)
+            nc.vector.quantize_mx(out=codes[:].bitcast(FP8X4), scales=scales[:], in_=values)
+            return codes, scales
+
+        xq, wq = [], []
+        for i in range(2):
+            xq.append(quantize(f"x{i}", grouped[i][:]))
+            wq.append(quantize(f"w{i}", w_grouped[i][:].rearrange("p n j -> p (n j)")))
+
+        products = [(0, 0, 0, 256, "s"), (0, 1, 0, 256, "s"), (1, 0, 0, 256, "v"), (1, 1, 0, 128, "s"), (1, 1, 128, 256, "v")]
+        for i, (m, c, c0, c1, engine) in enumerate(products):
+            rows = slice(m * M_TILE, (m + 1) * M_TILE)
+            v0 = CHUNKS[c][0]
+            acc = psum.tile([M_TILE, c1 - c0], F32, name=f"acc{i}")
+            nc.tensor.matmul_mx(
+                out=acc[:],
+                lhsT=wq[m][0][:].bitcast(FP8X4),
+                lhsT_scale=wq[m][1][:],
+                rhs=xq[c][0][:, c0:c1].bitcast(FP8X4),
+                rhs_scale=xq[c][1][:, c0:c1],
+                start=True,
+                stop=True,
+            )
+            result = keep.tile([M_TILE, c1 - c0], F32, name=f"result{i}")
+            if engine == "v":
+                nc.vector.tensor_scalar(result[:], acc[:], bias[:, m : m + 1], 0.0, ADD, MAX)
+            else:
+                nc.scalar.activation(result[:], acc[:], RELU, bias=bias[:, m : m + 1])
+            nc.sync.dma_start(out[rows, v0 + c0 : v0 + c1], result[:])

@@ -1,6 +1,7 @@
 from contextlib import ExitStack
 
 import concourse.mybir as mybir
+from concourse.masks import make_identity
 
 K, T, LEVELS, V, N = 512, 1024, 4, 512, 256
 FLOPS = 2 * K * V * N
@@ -46,16 +47,21 @@ def tile_picked_grid_lin_relu_sub_l_kernel(tc, xT, w, b, offs, out):
         tables = [keep.tile([P, T], F32, name=f"table{l}") for l in range(LEVELS)]
         w_raw = keep.tile([P, PACK, N], F32, name="w_raw")
         bias = keep.tile([P, N // M_TILE], F32, name="bias")
-        for l in range(LEVELS):
+        bias_rows = keep.tile([P, P], F32, name="bias_rows")
+        nc.vector.memset(bias_rows[:], 0.0)
+        nc.sync.dma_start(tables[0][:], levels[0])
+        nc.sync.dma_start(bias_rows[0:2, :], b.rearrange("(c p) o -> c (p o)", p=P))
+        for l in range(1, LEVELS):
             nc.sync.dma_start(tables[l][:], levels[l])
         nc.sync.dma_start(w_raw[:], w.rearrange("(p j) n -> p j n", j=PACK))
-        with nc.allow_non_contiguous_dma(reason="one bias value a partition"):
-            nc.sync.dma_start(bias[:], b.rearrange("(c p) o -> p (c o)", p=P))
 
-        zero = keep.tile([P, 1], F32, name="zero")
+        identity = keep.tile([P, P], F32, name="identity")
         warm = keep.tile([P, 1], F32, name="warm")
-        nc.vector.memset(zero[:], 0.0)
-        nc.scalar.activation(warm[:], zero[:], RELU)
+        make_identity(nc, identity[:])
+        nc.scalar.activation(warm[:], identity[:, 0:1], RELU)
+        bias_turned = psum.tile([P, P], F32, name="bias_turned")
+        nc.tensor.transpose(bias_turned[:], bias_rows[:], identity[:])
+        nc.scalar.copy(bias[:], bias_turned[:, 0:2])
 
         pairs = keep.tile([P, 2, V, 2], BF16, name="pairs")
         for l in range(2):
@@ -63,25 +69,25 @@ def tile_picked_grid_lin_relu_sub_l_kernel(tc, xT, w, b, offs, out):
             nc.vector.tensor_copy(rounded[:], tables[l][:])
             nc.scalar.activation(pairs[:, 0, :, l], rounded[:].indirect(level_offsets(l, 0, V)), COPY)
         nc.vector.tensor_copy(pairs[:, 1, :, 0], tables[2][:].indirect(level_offsets(2, 0, V)))
-        for v0, v1 in CHUNKS:
-            l = LEVELS - 1
-            nc.vector.tensor_copy(pairs[:, l // 2, v0:v1, l % 2], tables[l][:].indirect(level_offsets(l, v0, v1)))
+
+        def gather_last(v0, v1):
+            nc.vector.tensor_copy(pairs[:, 1, v0:v1, 1], tables[3][:].indirect(level_offsets(3, v0, v1)))
+
         pair_words = pairs[:].rearrange("p u v e -> p u (v e)").bitcast(I32)
 
-        grouped = []
-        for c, (v0, v1) in enumerate(CHUNKS):
-            g = keep.tile([P, (v1 - v0) * PACK], BF16, name=f"grouped{c}", align_bytes=64)
+        staged = keep.tile([P, V + N, PACK], BF16, name="staged", align_bytes=64)
+        w_at = {1: 0, 0: 384}
+        x_at = {0: 128, 256: 512, 384: 640}
+        nc.scalar.copy(*interleave_views(staged[:, 384 : 512 + 4, :], w_raw[:, :, 0 : M_TILE + 4]))
+        nc.scalar.copy(*interleave_views(staged[:, 0:128, :], w_raw[:, :, M_TILE:N]))
+        flat = staged[:].rearrange("p n j -> p (n j)")
+        words = flat.bitcast(I32)
+
+        def interleave(v0, v1):
             nc.vector.tensor_copy(
-                g[:].bitcast(I32).rearrange("p (c i u) -> p c u i", i=4, u=2),
+                words[:, 2 * x_at[v0] : 2 * (x_at[v0] + v1 - v0)].rearrange("p (c i u) -> p c u i", i=4, u=2),
                 pair_words[:, :, v0:v1].rearrange("p u (c i) -> p c u i", i=4),
             )
-            grouped.append(g)
-
-        w_grouped = []
-        for m in range(N // M_TILE):
-            g = keep.tile([P, M_TILE, PACK], BF16, name=f"w_grouped{m}", align_bytes=64)
-            nc.scalar.copy(*interleave_views(g[:], w_raw[:, :, m * M_TILE : (m + 1) * M_TILE]))
-            w_grouped.append(g)
 
         def quantize(name, values):
             n = values.shape[1] // PACK
@@ -90,28 +96,43 @@ def tile_picked_grid_lin_relu_sub_l_kernel(tc, xT, w, b, offs, out):
             nc.vector.quantize_mx(out=codes[:].bitcast(FP8X4), scales=scales[:], in_=values)
             return codes, scales
 
-        xq, wq = [], []
-        for i in range(2):
-            xq.append(quantize(f"x{i}", grouped[i][:]))
-            wq.append(quantize(f"w{i}", w_grouped[i][:].rearrange("p n j -> p (n j)")))
+        def quantize_x(v0, v1):
+            return quantize(f"x{v0}", flat[:, x_at[v0] * PACK : (x_at[v0] + v1 - v0) * PACK])
 
-        products = [(0, 0, 0, 256, "s"), (0, 1, 0, 256, "s"), (1, 0, 0, 256, "v"), (1, 1, 0, 128, "s"), (1, 1, 128, 256, "v")]
-        for i, (m, c, c0, c1, engine) in enumerate(products):
-            rows = slice(m * M_TILE, (m + 1) * M_TILE)
-            v0 = CHUNKS[c][0]
-            acc = psum.tile([M_TILE, c1 - c0], F32, name=f"acc{i}")
+        def quantize_w(m):
+            return quantize(f"w{m}", flat[:, w_at[m] * PACK : (w_at[m] + M_TILE) * PACK])
+
+        def product(m, wq, xq, v0, v1, on_vector):
+            acc = psum.tile([M_TILE, v1 - v0], F32, name=f"acc{m}_{v0}")
             nc.tensor.matmul_mx(
                 out=acc[:],
-                lhsT=wq[m][0][:].bitcast(FP8X4),
-                lhsT_scale=wq[m][1][:],
-                rhs=xq[c][0][:, c0:c1].bitcast(FP8X4),
-                rhs_scale=xq[c][1][:, c0:c1],
+                lhsT=wq[0][:].bitcast(FP8X4),
+                lhsT_scale=wq[1][:],
+                rhs=xq[0][:].bitcast(FP8X4),
+                rhs_scale=xq[1][:],
                 start=True,
                 stop=True,
             )
-            result = keep.tile([M_TILE, c1 - c0], F32, name=f"result{i}")
-            if engine == "v":
+            result = keep.tile([M_TILE, v1 - v0], F32, name=f"result{m}_{v0}")
+            if on_vector:
                 nc.vector.tensor_scalar(result[:], acc[:], bias[:, m : m + 1], 0.0, ADD, MAX)
             else:
                 nc.scalar.activation(result[:], acc[:], RELU, bias=bias[:, m : m + 1])
-            nc.sync.dma_start(out[rows, v0 + c0 : v0 + c1], result[:])
+            nc.sync.dma_start(out[m * M_TILE : (m + 1) * M_TILE, v0:v1], result[:])
+
+        gather_last(0, 256 + GROUP)
+        gather_last(384, 512)
+        interleave(0, 256)
+        gather_last(256, 384)
+        xa = quantize_x(0, 256)
+        w0 = quantize_w(0)
+        interleave(256, 512)
+        w1 = quantize_w(1)
+        xb = quantize_x(256, 384)
+        xc = quantize_x(384, 512)
+        product(0, w0, xa, 0, 256, False)
+        product(1, w1, xa, 0, 256, False)
+        product(0, w0, xb, 256, 384, False)
+        product(1, w1, xb, 256, 384, True)
+        product(0, w0, xc, 384, 512, False)
+        product(1, w1, xc, 384, 512, True)

from contextlib import ExitStack

import concourse.mybir as mybir
from concourse.masks import make_identity

K, T, LEVELS, V, N = 512, 1024, 4, 512, 256
FLOPS = 2 * K * V * N

F32 = mybir.dt.float32
BF16 = mybir.dt.bfloat16
U32 = mybir.dt.uint32
I32 = mybir.dt.int32
U16 = mybir.dt.uint16
U8 = mybir.dt.uint8
FP8X4 = mybir.dt.float8_e4m3fn_x4
RELU = mybir.ActivationFunctionType.Relu
COPY = mybir.ActivationFunctionType.Copy
ADD, MAX = mybir.AluOpType.add, mybir.AluOpType.max

P = 128
PACK = 4
M_TILE = 128
GROUP = 16
CHUNKS = [(0, 256), (256, 512)]


def interleave_views(dst, src):
    return (
        dst.rearrange("p (c i) t -> p c t i", i=4),
        src.rearrange("p t (c i) -> p c t i", i=4),
    )


def tile_picked_grid_lin_relu_sub_l_kernel(tc, xT, w, b, offs, out):
    nc = tc.nc
    with ExitStack() as ctx:
        keep = ctx.enter_context(tc.tile_pool(name="keep", bufs=1))
        psum = ctx.enter_context(tc.psum_pool(name="psum", bufs=1))

        offsets = keep.tile([P, LEVELS * V // GROUP], U16, name="offsets")
        nc.sync.dma_start(offsets[:], offs)

        def level_offsets(level, v0, v1):
            return offsets[:, (level * V + v0) // GROUP : (level * V + v1) // GROUP]

        levels = xT.rearrange("(f l) t -> l f t", l=LEVELS)
        tables = [keep.tile([P, T], F32, name=f"table{l}") for l in range(LEVELS)]
        w_raw = keep.tile([P, PACK, N], F32, name="w_raw")
        bias = keep.tile([P, N // M_TILE], F32, name="bias")
        bias_rows = keep.tile([P, P], F32, name="bias_rows")
        nc.vector.memset(bias_rows[:], 0.0)
        nc.sync.dma_start(tables[0][:], levels[0])
        nc.sync.dma_start(bias_rows[0:2, :], b.rearrange("(c p) o -> c (p o)", p=P))
        for l in range(1, LEVELS):
            nc.sync.dma_start(tables[l][:], levels[l])
        nc.sync.dma_start(w_raw[:], w.rearrange("(p j) n -> p j n", j=PACK))

        identity = keep.tile([P, P], F32, name="identity")
        warm = keep.tile([P, 1], F32, name="warm")
        make_identity(nc, identity[:])
        nc.scalar.activation(warm[:], identity[:, 0:1], RELU)
        bias_turned = psum.tile([P, P], F32, name="bias_turned")
        nc.tensor.transpose(bias_turned[:], bias_rows[:], identity[:])
        nc.scalar.copy(bias[:], bias_turned[:, 0:2])

        pairs = keep.tile([P, 2, V, 2], BF16, name="pairs")
        for l in range(2):
            rounded = keep.tile([P, T], BF16, name=f"rounded{l}")
            nc.vector.tensor_copy(rounded[:], tables[l][:])
            nc.scalar.activation(pairs[:, 0, :, l], rounded[:].indirect(level_offsets(l, 0, V)), COPY)
        nc.vector.tensor_copy(pairs[:, 1, :, 0], tables[2][:].indirect(level_offsets(2, 0, V)))

        def gather_last(v0, v1):
            nc.vector.tensor_copy(pairs[:, 1, v0:v1, 1], tables[3][:].indirect(level_offsets(3, v0, v1)))

        pair_words = pairs[:].rearrange("p u v e -> p u (v e)").bitcast(I32)

        staged = keep.tile([P, V + N, PACK], BF16, name="staged", align_bytes=64)
        w_at = {1: 0, 0: 384}
        x_at = {0: 128, 256: 512, 384: 640}
        nc.scalar.copy(*interleave_views(staged[:, 384 : 512 + 4, :], w_raw[:, :, 0 : M_TILE + 4]))
        nc.scalar.copy(*interleave_views(staged[:, 0:128, :], w_raw[:, :, M_TILE:N]))
        flat = staged[:].rearrange("p n j -> p (n j)")
        words = flat.bitcast(I32)

        def interleave(v0, v1):
            nc.vector.tensor_copy(
                words[:, 2 * x_at[v0] : 2 * (x_at[v0] + v1 - v0)].rearrange("p (c i u) -> p c u i", i=4, u=2),
                pair_words[:, :, v0:v1].rearrange("p u (c i) -> p c u i", i=4),
            )

        def quantize(name, values):
            n = values.shape[1] // PACK
            codes = keep.tile([P, n], U32, name=f"{name}_codes", align_bytes=64)
            scales = keep.tile([P, n], U8, name=f"{name}_scales", align_bytes=64)
            nc.vector.quantize_mx(out=codes[:].bitcast(FP8X4), scales=scales[:], in_=values)
            return codes, scales

        def quantize_x(v0, v1):
            return quantize(f"x{v0}", flat[:, x_at[v0] * PACK : (x_at[v0] + v1 - v0) * PACK])

        def quantize_w(m):
            return quantize(f"w{m}", flat[:, w_at[m] * PACK : (w_at[m] + M_TILE) * PACK])

        def product(m, wq, xq, v0, v1, on_vector):
            acc = psum.tile([M_TILE, v1 - v0], F32, name=f"acc{m}_{v0}")
            nc.tensor.matmul_mx(
                out=acc[:],
                lhsT=wq[0][:].bitcast(FP8X4),
                lhsT_scale=wq[1][:],
                rhs=xq[0][:].bitcast(FP8X4),
                rhs_scale=xq[1][:],
                start=True,
                stop=True,
            )
            result = keep.tile([M_TILE, v1 - v0], F32, name=f"result{m}_{v0}")
            if on_vector:
                nc.vector.tensor_scalar(result[:], acc[:], bias[:, m : m + 1], 0.0, ADD, MAX)
            else:
                nc.scalar.activation(result[:], acc[:], RELU, bias=bias[:, m : m + 1])
            nc.sync.dma_start(out[m * M_TILE : (m + 1) * M_TILE, v0:v1], result[:])

        gather_last(0, 256 + GROUP)
        gather_last(384, 512)
        interleave(0, 256)
        gather_last(256, 384)
        xa = quantize_x(0, 256)
        w0 = quantize_w(0)
        interleave(256, 512)
        w1 = quantize_w(1)
        xb = quantize_x(256, 384)
        xc = quantize_x(384, 512)
        product(0, w0, xa, 0, 256, False)
        product(1, w1, xa, 0, 256, False)
        product(0, w0, xb, 256, 384, False)
        product(1, w1, xb, 256, 384, True)
        product(0, w0, xc, 384, 512, False)
        product(1, w1, xc, 384, 512, True)
